import numpy as np, ml_dtypes
CORES = [24,32,56,88,96,104,30,38,62,94,102,110]
N = 12
import mx_ref
NC = 128
BF = ml_dtypes.bfloat16
def setup_inputs(rng):
    def f(*shape):
        return mx_ref.flush((rng.standard_normal(shape, dtype=np.float32) * np.exp2(rng.integers(-2, 3, shape[:-1] + (1,)))).astype(BF))
    return {"u": f(N, 128, 512), "v": f(N, 128, 512), "x": f(N, 128, 4 * NC)}
def setup_inputs_blocks(rng):
    d = setup_inputs(rng)
    for k in ("u", "v", "x"): d[k] = mx_ref.spread(d[k], rng, 4)
    return d
def setup_inputs_wide(rng):
    d = setup_inputs(rng)
    for k in ("u", "v", "x"): d[k] = mx_ref.flush((d[k].astype(np.float32) * np.exp2(rng.integers(-8, 9, (N, 1, 1))).astype(np.float32)).astype(BF))
    return d
def setup_inputs_zeros(rng):
    d = setup_inputs(rng); v = d["x"].reshape(N, 128, -1, 4).copy()
    v[np.broadcast_to((rng.random((N, 1, v.shape[2], 1)) < 0.33), v.shape)] = 0
    d["x"] = v.reshape(d["x"].shape)
    return d
def reference(u, v, x):
    QX = [mx_ref.quantize(x[j]) for j in range(N)]
    y = np.zeros((N, 128, N * NC), np.float32)
    for r in range(N):
        qu, qv = mx_ref.quantize(u[r]), mx_ref.quantize(v[r])
        for j in range(N):
            y[r][:, NC * j:NC * j + NC] = np.maximum(mx_ref.matmul(qu, QX[j]), np.float32(0)) * mx_ref.matmul(qv, QX[j])
    return {"y": y}

@@ -1,0 +1,186 @@
+from concourse.bass import DstId, RemoteDMATransfer
+from concourse.mybir import dt, AluOpType, ActivationFunctionType
+
+N = 12
+NC = 128
+SIM_CORES = 112
+BANK = 512
+NBANKS = 8
+HELP_START = 4.0
+HELP_STEP = 0.5
+FLUSH = (2, 4, 6, 8, 10, 11, 12)
+
+SCRATCH = {
+    "xb": ("sbuf", [128, 4 * NC], "bfloat16"),
+    "ub": ("sbuf", [128, 512], "bfloat16"),
+    "vb": ("sbuf", [128, 512], "bfloat16"),
+    "qx": ("sbuf", [128, N * NC], "float8_e4m3fn_x4"),
+    "sx": ("sbuf", [128, N * NC], "uint8"),
+    "qu": ("sbuf", [128, 128], "float8_e4m3fn_x4"),
+    "su": ("sbuf", [128, 128], "uint8"),
+    "qv": ("sbuf", [128, 128], "float8_e4m3fn_x4"),
+    "sv": ("sbuf", [128, 128], "uint8"),
+    "rl": ("sbuf", [128, N * NC], "float32"),
+    "yb": ("sbuf", [128, N * NC], "float32"),
+    "ps": ("psum", [128, NBANKS * BANK], "float32"),
+}
+SEMAPHORES = (["ldx", "ldu", "ldv", "qx", "qw", "sent", "st"]
+              + ["t%d" % j for j in range(N)]
+              + ["mu%d" % p for p in range(N)] + ["mv%d" % p for p in range(N)]
+              + ["rs%d" % p for p in range(N)] + ["ml%d" % p for p in range(N)])
+
+
+def _count(mask):
+    return bin(mask).count("1")
+
+
+def make_plan(cores, topo):
+    group = set(cores)
+    chips = sorted({topo.chip(c) for c in cores})
+    ranks_on = {ch: [c for c in cores if topo.chip(c) == ch] for ch in chips}
+    steps, arrive, eta = {}, {}, {}
+    for j, s in enumerate(cores):
+        home = topo.chip(s)
+        hi = chips.index(home)
+        others = [ch for ch in chips if ch != home]
+        spare = [c for c in range(SIM_CORES)
+                 if topo.chip(c) == home and c not in group and topo.die(c) == topo.die(s)]
+
+        def able(c, ch):
+            return all(topo.may_write(c, r) for r in ranks_on[ch])
+
+        others.sort(key=lambda ch: (sum(able(c, ch) for c in [s] + spare), (chips.index(ch) - hi) % len(chips)))
+        busy = {s: 0.0}
+        load = {s: []}
+        for ch in others:
+            best = None
+            for c in [s] + spare:
+                if not able(c, ch):
+                    continue
+                start = busy[c] if c in busy else HELP_START + HELP_STEP * (len(busy) - 1)
+                if best is None or start + 2 < best[0]:
+                    best = (start + 2, c)
+            busy[best[1]] = best[0]
+            load.setdefault(best[1], []).append(ch)
+        helpers = sorted([c for c in load if c != s], key=lambda c: -len(load[c]))
+        mates_here = [r for r in ranks_on[home] if r != s]
+        far = ranks_on[others[0]][0]
+        near = (helpers + mates_here)[0]
+        off = topo.mask(s, far)
+        stay = topo.mask(s, near) & ~off
+        local = ([helpers] if helpers else []) + ([mates_here] if mates_here else [])
+        mine = sorted(load[s], key=lambda ch: (chips.index(ch) - hi) % len(chips))
+        for k in range(max(len(mine), len(local))):
+            tr = []
+            if k < len(mine):
+                tr.append((off, list(ranks_on[mine[k]])))
+                for r in ranks_on[mine[k]]:
+                    eta.setdefault(r, {})[j] = 2.0 * (k + 1)
+            if k < len(local):
+                tr.append((stay, list(local[k])))
+                for r in local[k]:
+                    eta.setdefault(r, {})[j] = 1.0 + k
+            steps.setdefault(s, []).append((j, tr))
+        eta.setdefault(s, {})[j] = -1.0
+        for i, h in enumerate(helpers):
+            todo = sorted(load[h], key=lambda ch: (chips.index(ch) - hi) % len(chips))
+            for k, ch in enumerate(todo):
+                steps.setdefault(h, []).append((j, [(topo.mask(h, ranks_on[ch][0]), list(ranks_on[ch]))]))
+                for r in ranks_on[ch]:
+                    eta.setdefault(r, {})[j] = HELP_START + HELP_STEP * i + 2.0 * (k + 1)
+    for c in steps:
+        for j, tr in steps[c]:
+            for mask, dsts in tr:
+                for d in dsts:
+                    arrive.setdefault(d, {})[j] = 2 * _count(mask)
+    return steps, arrive, eta
+
+
+def _send(g, T, topo, todo, own, arrive):
+    total = 0
+    waited = set()
+    for j, tr in todo:
+        if j != own and j not in waited:
+            g.wait_ge(T.sem["t%d" % j], arrive[j])
+            waited.add(j)
+        a, b = j * NC, (j + 1) * NC
+        for ap in (T.qx[:, a:b].bitcast(dt.uint8), T.sx[:, a:b]):
+            calls = []
+            for mask, dsts in tr:
+                ids = []
+                for d in dsts:
+                    rid, pid, _ = topo.addr(d)
+                    ids.append(DstId(rid=rid, pnc=pid))
+                calls.append(RemoteDMATransfer(dst_ids=ids, dma_engine_mask=mask, remote_sem=T.sem["t%d" % j],
+                                               srcs=[ap], dsts=[ap for _ in dsts]))
+                total += _count(mask)
+            g.remote_dma_fused(calls, local_sem=T.sem.sent)
+    if total:
+        g.wait_ge(T.sem.sent, total)
+
+
+def rank_program(g, core, T, topo):
+    steps, arrive, eta = make_plan(list(T.cores), topo)
+    me = T.rank_of(core)
+    if me is None:
+        if core in steps:
+            _send(g, T, topo, steps[core], None, arrive[core])
+        return
+    S = T.sem
+    own = slice(me * NC, (me + 1) * NC)
+
+    g.sync.dma_start(T.xb[:], T.x[:]).then_inc(S.ldx, 16)
+    g.scalar.dma_start(T.ub[:], T.u[:]).then_inc(S.ldu, 16)
+    g.sync.dma_start(T.vb[:], T.v[:]).then_inc(S.ldv, 16)
+    g.vector.wait_ge(S.ldx, 16)
+    g.vector.quantize_mx(T.qx[:, own], T.sx[:, own], T.xb[:]).then_inc(S.qx, 1)
+    g.vector.wait_ge(S.ldu, 16)
+    g.vector.quantize_mx(T.qu[:], T.su[:], T.ub[:]).then_inc(S.qw, 1)
+    g.vector.wait_ge(S.ldv, 16)
+    g.vector.quantize_mx(T.qv[:], T.sv[:], T.vb[:]).then_inc(S.qw, 1)
+
+    g.wait_ge(S.qx, 1)
+    _send(g, T, topo, steps[core], me, arrive[core])
+
+    order = sorted(range(N), key=lambda j: (eta[core][j], j))
+    g.tensor.wait_ge(S.qw, 2)
+    for p, j in enumerate(order):
+        cols = slice(j * NC, (j + 1) * NC)
+        pos = slice(p * NC, (p + 1) * NC)
+        bu = ((2 * p) % NBANKS) * BANK
+        bv = ((2 * p + 1) % NBANKS) * BANK
+        if j == me:
+            g.tensor.wait_ge(S.qx, 1)
+        else:
+            g.tensor.wait_ge(S["t%d" % j], arrive[core][j])
+        if 2 * p >= NBANKS:
+            g.tensor.wait_ge(S["ml%d" % (p - NBANKS // 2)], 1)
+        g.tensor.matmul_mx(T.ps[:, bu:bu + NC], T.qu[:], T.su[:], T.qx[:, cols], T.sx[:, cols],
+                           True, True).then_inc(S["mu%d" % p], 1)
+        g.tensor.matmul_mx(T.ps[:, bv:bv + NC], T.qv[:], T.sv[:], T.qx[:, cols], T.sx[:, cols],
+                           True, True).then_inc(S["mv%d" % p], 1)
+        g.scalar.wait_ge(S["mu%d" % p], 1)
+        g.scalar.activation(T.rl[:, pos], T.ps[:, bu:bu + NC], ActivationFunctionType.Relu).then_inc(S["rs%d" % p], 1)
+        g.vector.wait_ge(S["mv%d" % p], 1)
+        g.vector.wait_ge(S["rs%d" % p], 1)
+        g.vector.tensor_tensor(T.yb[:, cols], T.rl[:, pos], T.ps[:, bv:bv + NC], AluOpType.mult).then_inc(S["ml%d" % p], 1)
+
+    stores = 0
+    done = 0
+    for upto in FLUSH:
+        for p in range(done, upto):
+            g.sync.wait_ge(S["ml%d" % p], 1)
+        blocks = sorted(order[done:upto])
+        done = upto
+        run = [blocks[0], blocks[0]]
+        runs = [run]
+        for j in blocks[1:]:
+            if j == run[1] + 1:
+                run[1] = j
+            else:
+                run = [j, j]
+                runs.append(run)
+        for lo, hi in runs:
+            g.sync.dma_start(T.y[:, lo * NC:(hi + 1) * NC], T.yb[:, lo * NC:(hi + 1) * NC]).then_inc(S.st, 16)
+            stores += 1
+    g.sync.wait_ge(S.st, 16 * stores)

@@ -6,8 +6,7 @@ NC = 128
 SIM_CORES = 112
 BANK = 512
 NBANKS = 8
-HELP_START = 4.0
-HELP_STEP = 0.5
+LAT = 0.7
 FLUSH = (2, 4, 6, 8, 10, 11, 12)
 
 SCRATCH = {
@@ -24,7 +23,7 @@ SCRATCH = {
     "yb": ("sbuf", [128, N * NC], "float32"),
     "ps": ("psum", [128, NBANKS * BANK], "float32"),
 }
-SEMAPHORES = (["ldx", "ldu", "ldv", "qx", "qw", "sent", "st"]
+SEMAPHORES = (["ldx", "ldu", "ldv", "qx", "qw", "sent", "st", "fs", "fc"]
               + ["t%d" % j for j in range(N)]
               + ["mu%d" % p for p in range(N)] + ["mv%d" % p for p in range(N)]
               + ["rs%d" % p for p in range(N)] + ["ml%d" % p for p in range(N)])
@@ -38,80 +37,134 @@ def make_plan(cores, topo):
     group = set(cores)
     chips = sorted({topo.chip(c) for c in cores})
     ranks_on = {ch: [c for c in cores if topo.chip(c) == ch] for ch in chips}
-    steps, arrive, eta = {}, {}, {}
+    acts, arrive, eta, feed, free = {}, {}, {}, {}, {}
+    fwd = {c: [] for c in cores}
+
+    def peer(ch, d):
+        return [r for r in ranks_on[ch] if topo.die(r) == d][0]
+
     for j, s in enumerate(cores):
         home = topo.chip(s)
         hi = chips.index(home)
+        d = topo.die(s)
         others = [ch for ch in chips if ch != home]
         spare = [c for c in range(SIM_CORES)
-                 if topo.chip(c) == home and c not in group and topo.die(c) == topo.die(s)]
+                 if topo.chip(c) == home and c not in group and topo.die(c) == d]
+
+        def ring(ch):
+            return (chips.index(ch) - hi) % len(chips)
 
         def able(c, ch):
             return all(topo.may_write(c, r) for r in ranks_on[ch])
 
-        others.sort(key=lambda ch: (sum(able(c, ch) for c in [s] + spare), (chips.index(ch) - hi) % len(chips)))
-        busy = {s: 0.0}
+        others.sort(key=lambda ch: (sum(able(c, ch) for c in [s] + spare), ring(ch)))
         load = {s: []}
         for ch in others:
             best = None
             for c in [s] + spare:
-                if not able(c, ch):
+                if not able(c, ch) or (c not in load and len(load) > 2):
                     continue
-                start = busy[c] if c in busy else HELP_START + HELP_STEP * (len(busy) - 1)
-                if best is None or start + 2 < best[0]:
-                    best = (start + 2, c)
-            busy[best[1]] = best[0]
+                start = 0.0 if c == s else 2.0 + LAT + (0.1 * (len(load) - 1) if c not in load else 0.0)
+                t = start + len(load.get(c, [])) + 2
+                if best is None or t < best[0]:
+                    best = (t, c)
             load.setdefault(best[1], []).append(ch)
         helpers = sorted([c for c in load if c != s], key=lambda c: -len(load[c]))
-        mates_here = [r for r in ranks_on[home] if r != s]
-        far = ranks_on[others[0]][0]
-        near = (helpers + mates_here)[0]
-        off = topo.mask(s, far)
-        stay = topo.mask(s, near) & ~off
-        local = ([helpers] if helpers else []) + ([mates_here] if mates_here else [])
-        mine = sorted(load[s], key=lambda ch: (chips.index(ch) - hi) % len(chips))
-        for k in range(max(len(mine), len(local))):
-            tr = []
-            if k < len(mine):
-                tr.append((off, list(ranks_on[mine[k]])))
-                for r in ranks_on[mine[k]]:
-                    eta.setdefault(r, {})[j] = 2.0 * (k + 1)
-            if k < len(local):
-                tr.append((stay, list(local[k])))
-                for r in local[k]:
-                    eta.setdefault(r, {})[j] = 1.0 + k
-            steps.setdefault(s, []).append((j, tr))
+        partner = [r for r in ranks_on[home] if r != s][0]
+        off = topo.mask(s, ranks_on[others[0]][0])
+        stay = topo.mask(s, partner) & ~off
+
+        def route(c, t):
+            todo = sorted(load[c], key=ring)
+            last = max(todo, key=lambda ch: (len(fwd[peer(ch, d)]), ring(ch)))
+            out = []
+            for ch in todo:
+                if ch == last:
+                    continue
+                r = peer(ch, d)
+                t += 1
+                out.append([r])
+                eta.setdefault(r, {})[j] = t
+                fwd[r].append(j)
+            two = list(ranks_on[last])
+            if (j + chips.index(last)) % 2:
+                two.reverse()
+            for r in two:
+                t += 1
+                eta.setdefault(r, {})[j] = t
+            out.append(two)
+            return out, t
+
         eta.setdefault(s, {})[j] = -1.0
-        for i, h in enumerate(helpers):
-            todo = sorted(load[h], key=lambda ch: (chips.index(ch) - hi) % len(chips))
-            for k, ch in enumerate(todo):
-                steps.setdefault(h, []).append((j, [(topo.mask(h, ranks_on[ch][0]), list(ranks_on[ch]))]))
-                for r in ranks_on[ch]:
-                    eta.setdefault(r, {})[j] = HELP_START + HELP_STEP * i + 2.0 * (k + 1)
-    for c in steps:
-        for j, tr in steps[c]:
+        mine = acts.setdefault(s, [])
+        if len(load[s]) <= 1 and len(helpers) == 2:
+            mine.append((j, None, [(off, [helpers[0]]), (stay, [helpers[1]])]))
+            fed = 1.0
+            out, t = route(s, fed)
+            mine.append((j, None, [(off, out[0]), (stay, [partner])]))
+            eta.setdefault(partner, {})[j] = fed + 1
+            free[s] = (t, fed + 1)
+            carry = None
+        else:
+            fed = float(len(helpers))
+            out, t = route(s, 0.0)
+            for k, ds in enumerate(out):
+                mine.append((j, None, [(off, ds)] + ([(stay, helpers)] if k == 0 else [])))
+            free[s] = (t, fed)
+            carry = helpers[0]
+        for h in helpers:
+            out, t = route(h, fed + LAT)
+            for k, ds in enumerate(out):
+                tr = [(off, ds)]
+                if k == 0 and h == carry:
+                    tr.append((stay, [partner]))
+                    eta.setdefault(partner, {})[j] = fed + LAT + 1
+                acts.setdefault(h, []).append((j, "parts" if k == 0 else None, tr))
+
+    for r in cores:
+        partner = [c for c in ranks_on[topo.chip(r)] if c != r][0]
+        far = [c for c in cores if topo.chip(c) != topo.chip(r)][0]
+        full = topo.mask(r, partner)
+        stay = full & ~topo.mask(r, far)
+        t0, t1 = free[r]
+        for k, j in enumerate(sorted(fwd[r], key=lambda i: eta[r][i])):
+            if k < 2:
+                t1 = max(eta[r][j] + LAT, t1) + 1
+                mask, t = stay, t1
+            else:
+                t0 = t1 = max(eta[r][j] + LAT, t0, t1) + 0.5
+                mask, t = full, t0
+            acts[r].append((j, "tile", [(mask, [partner])]))
+            eta[partner][j] = t
+    for c in acts:
+        for j, wait, tr in acts[c]:
             for mask, dsts in tr:
-                for d in dsts:
-                    arrive.setdefault(d, {})[j] = 2 * _count(mask)
-    return steps, arrive, eta
+                for x in dsts:
+                    if x in group:
+                        arrive.setdefault(x, {})[j] = 2 * _count(mask)
+                    else:
+                        feed[x] = _count(mask)
+    return acts, arrive, eta, feed
 
 
-def _send(g, T, topo, todo, own, arrive):
+def _send(g, T, topo, todo, arrive, fed):
+    group = set(T.cores)
     total = 0
-    waited = set()
-    for j, tr in todo:
-        if j != own and j not in waited:
-            g.wait_ge(T.sem["t%d" % j], arrive[j])
-            waited.add(j)
+    for j, wait, tr in todo:
         a, b = j * NC, (j + 1) * NC
-        for ap in (T.qx[:, a:b].bitcast(dt.uint8), T.sx[:, a:b]):
+        if wait == "tile":
+            g.wait_ge(T.sem["t%d" % j], arrive[j])
+        for ap, part in ((T.sx[:, a:b], "fs"), (T.qx[:, a:b].bitcast(dt.uint8), "fc")):
+            if wait == "parts":
+                g.wait_ge(T.sem[part], fed)
             calls = []
             for mask, dsts in tr:
                 ids = []
-                for d in dsts:
-                    rid, pid, _ = topo.addr(d)
+                for x in dsts:
+                    rid, pid, _ = topo.addr(x)
                     ids.append(DstId(rid=rid, pnc=pid))
-                calls.append(RemoteDMATransfer(dst_ids=ids, dma_engine_mask=mask, remote_sem=T.sem["t%d" % j],
+                sem = T.sem["t%d" % j] if dsts[0] in group else T.sem[part]
+                calls.append(RemoteDMATransfer(dst_ids=ids, dma_engine_mask=mask, remote_sem=sem,
                                                srcs=[ap], dsts=[ap for _ in dsts]))
                 total += _count(mask)
             g.remote_dma_fused(calls, local_sem=T.sem.sent)
@@ -120,11 +173,11 @@ def _send(g, T, topo, todo, own, arrive):
 
 
 def rank_program(g, core, T, topo):
-    steps, arrive, eta = make_plan(list(T.cores), topo)
+    acts, arrive, eta, feed = make_plan(list(T.cores), topo)
     me = T.rank_of(core)
     if me is None:
-        if core in steps:
-            _send(g, T, topo, steps[core], None, arrive[core])
+        if core in acts:
+            _send(g, T, topo, acts[core], None, feed[core])
         return
     S = T.sem
     own = slice(me * NC, (me + 1) * NC)
@@ -140,7 +193,7 @@ def rank_program(g, core, T, topo):
     g.vector.quantize_mx(T.qv[:], T.sv[:], T.vb[:]).then_inc(S.qw, 1)
 
     g.wait_ge(S.qx, 1)
-    _send(g, T, topo, steps[core], me, arrive[core])
+    _send(g, T, topo, acts[core], arrive[core], None)
 
     order = sorted(range(N), key=lambda j: (eta[core][j], j))
     g.tensor.wait_ge(S.qw, 2)

@@ -40,9 +40,6 @@ def make_plan(cores, topo):
     acts, arrive, eta, feed, free = {}, {}, {}, {}, {}
     fwd = {c: [] for c in cores}
 
-    def peer(ch, d):
-        return [r for r in ranks_on[ch] if topo.die(r) == d][0]
-
     for j, s in enumerate(cores):
         home = topo.chip(s)
         hi = chips.index(home)
@@ -75,24 +72,14 @@ def make_plan(cores, topo):
         stay = topo.mask(s, partner) & ~off
 
         def route(c, t):
-            todo = sorted(load[c], key=ring)
-            last = max(todo, key=lambda ch: (len(fwd[peer(ch, d)]), ring(ch)))
             out = []
-            for ch in todo:
-                if ch == last:
-                    continue
-                r = peer(ch, d)
+            for ch in sorted(load[c], key=ring):
                 t += 1
+                r = min(ranks_on[ch], key=lambda x: (sum(1 for i in fwd[x] if abs(eta[x][i] - t) < 0.6),
+                                                     topo.die(x) != d))
                 out.append([r])
                 eta.setdefault(r, {})[j] = t
                 fwd[r].append(j)
-            two = list(ranks_on[last])
-            if (j + chips.index(last)) % 2:
-                two.reverse()
-            for r in two:
-                t += 1
-                eta.setdefault(r, {})[j] = t
-            out.append(two)
             return out, t
 
         eta.setdefault(s, {})[j] = -1.0
@@ -125,15 +112,17 @@ def make_plan(cores, topo):
         partner = [c for c in ranks_on[topo.chip(r)] if c != r][0]
         far = [c for c in cores if topo.chip(c) != topo.chip(r)][0]
         full = topo.mask(r, partner)
-        stay = full & ~topo.mask(r, far)
+        off = topo.mask(r, far)
+        stay = full & ~off
         t0, t1 = free[r]
-        for k, j in enumerate(sorted(fwd[r], key=lambda i: eta[r][i])):
-            if k < 2:
-                t1 = max(eta[r][j] + LAT, t1) + 1
-                mask, t = stay, t1
-            else:
-                t0 = t1 = max(eta[r][j] + LAT, t0, t1) + 0.5
-                mask, t = full, t0
+        for j in sorted(fwd[r], key=lambda i: (eta[r][i], i)):
+            ready = eta[r][j] + LAT
+            t, mask = min((max(ready, t1) + 1, 0, stay), (max(ready, t0) + 1, 1, off),
+                          (max(ready, t0, t1) + 0.5, 2, full))[::2]
+            if mask != off:
+                t1 = t
+            if mask != stay:
+                t0 = t
             acts[r].append((j, "tile", [(mask, [partner])]))
             eta[partner][j] = t
     for c in acts:

from concourse.bass import DstId, RemoteDMATransfer
from concourse.mybir import dt, AluOpType, ActivationFunctionType

N = 12
NC = 128
SIM_CORES = 112
BANK = 512
NBANKS = 8
LAT = 0.7
FLUSH = (2, 4, 6, 8, 10, 11, 12)

SCRATCH = {
    "xb": ("sbuf", [128, 4 * NC], "bfloat16"),
    "ub": ("sbuf", [128, 512], "bfloat16"),
    "vb": ("sbuf", [128, 512], "bfloat16"),
    "qx": ("sbuf", [128, N * NC], "float8_e4m3fn_x4"),
    "sx": ("sbuf", [128, N * NC], "uint8"),
    "qu": ("sbuf", [128, 128], "float8_e4m3fn_x4"),
    "su": ("sbuf", [128, 128], "uint8"),
    "qv": ("sbuf", [128, 128], "float8_e4m3fn_x4"),
    "sv": ("sbuf", [128, 128], "uint8"),
    "rl": ("sbuf", [128, N * NC], "float32"),
    "yb": ("sbuf", [128, N * NC], "float32"),
    "ps": ("psum", [128, NBANKS * BANK], "float32"),
}
SEMAPHORES = (["ldx", "ldu", "ldv", "qx", "qw", "sent", "st", "fs", "fc"]
              + ["t%d" % j for j in range(N)]
              + ["mu%d" % p for p in range(N)] + ["mv%d" % p for p in range(N)]
              + ["rs%d" % p for p in range(N)] + ["ml%d" % p for p in range(N)])


def _count(mask):
    return bin(mask).count("1")


def make_plan(cores, topo):
    group = set(cores)
    chips = sorted({topo.chip(c) for c in cores})
    ranks_on = {ch: [c for c in cores if topo.chip(c) == ch] for ch in chips}
    acts, arrive, eta, feed, free = {}, {}, {}, {}, {}
    fwd = {c: [] for c in cores}

    for j, s in enumerate(cores):
        home = topo.chip(s)
        hi = chips.index(home)
        d = topo.die(s)
        others = [ch for ch in chips if ch != home]
        spare = [c for c in range(SIM_CORES)
                 if topo.chip(c) == home and c not in group and topo.die(c) == d]

        def ring(ch):
            return (chips.index(ch) - hi) % len(chips)

        def able(c, ch):
            return all(topo.may_write(c, r) for r in ranks_on[ch])

        others.sort(key=lambda ch: (sum(able(c, ch) for c in [s] + spare), ring(ch)))
        load = {s: []}
        for ch in others:
            best = None
            for c in [s] + spare:
                if not able(c, ch) or (c not in load and len(load) > 2):
                    continue
                start = 0.0 if c == s else 2.0 + LAT + (0.1 * (len(load) - 1) if c not in load else 0.0)
                t = start + len(load.get(c, [])) + 2
                if best is None or t < best[0]:
                    best = (t, c)
            load.setdefault(best[1], []).append(ch)
        helpers = sorted([c for c in load if c != s], key=lambda c: -len(load[c]))
        partner = [r for r in ranks_on[home] if r != s][0]
        off = topo.mask(s, ranks_on[others[0]][0])
        stay = topo.mask(s, partner) & ~off

        def route(c, t):
            out = []
            for ch in sorted(load[c], key=ring):
                t += 1
                r = min(ranks_on[ch], key=lambda x: (sum(1 for i in fwd[x] if abs(eta[x][i] - t) < 0.6),
                                                     topo.die(x) != d))
                out.append([r])
                eta.setdefault(r, {})[j] = t
                fwd[r].append(j)
            return out, t

        eta.setdefault(s, {})[j] = -1.0
        mine = acts.setdefault(s, [])
        if len(load[s]) <= 1 and len(helpers) == 2:
            mine.append((j, None, [(off, [helpers[0]]), (stay, [helpers[1]])]))
            fed = 1.0
            out, t = route(s, fed)
            mine.append((j, None, [(off, out[0]), (stay, [partner])]))
            eta.setdefault(partner, {})[j] = fed + 1
            free[s] = (t, fed + 1)
            carry = None
        else:
            fed = float(len(helpers))
            out, t = route(s, 0.0)
            for k, ds in enumerate(out):
                mine.append((j, None, [(off, ds)] + ([(stay, helpers)] if k == 0 else [])))
            free[s] = (t, fed)
            carry = helpers[0]
        for h in helpers:
            out, t = route(h, fed + LAT)
            for k, ds in enumerate(out):
                tr = [(off, ds)]
                if k == 0 and h == carry:
                    tr.append((stay, [partner]))
                    eta.setdefault(partner, {})[j] = fed + LAT + 1
                acts.setdefault(h, []).append((j, "parts" if k == 0 else None, tr))

    for r in cores:
        partner = [c for c in ranks_on[topo.chip(r)] if c != r][0]
        far = [c for c in cores if topo.chip(c) != topo.chip(r)][0]
        full = topo.mask(r, partner)
        off = topo.mask(r, far)
        stay = full & ~off
        t0, t1 = free[r]
        for j in sorted(fwd[r], key=lambda i: (eta[r][i], i)):
            ready = eta[r][j] + LAT
            t, mask = min((max(ready, t1) + 1, 0, stay), (max(ready, t0) + 1, 1, off),
                          (max(ready, t0, t1) + 0.5, 2, full))[::2]
            if mask != off:
                t1 = t
            if mask != stay:
                t0 = t
            acts[r].append((j, "tile", [(mask, [partner])]))
            eta[partner][j] = t
    for c in acts:
        for j, wait, tr in acts[c]:
            for mask, dsts in tr:
                for x in dsts:
                    if x in group:
                        arrive.setdefault(x, {})[j] = 2 * _count(mask)
                    else:
                        feed[x] = _count(mask)
    return acts, arrive, eta, feed


def _send(g, T, topo, todo, arrive, fed):
    group = set(T.cores)
    total = 0
    for j, wait, tr in todo:
        a, b = j * NC, (j + 1) * NC
        if wait == "tile":
            g.wait_ge(T.sem["t%d" % j], arrive[j])
        for ap, part in ((T.sx[:, a:b], "fs"), (T.qx[:, a:b].bitcast(dt.uint8), "fc")):
            if wait == "parts":
                g.wait_ge(T.sem[part], fed)
            calls = []
            for mask, dsts in tr:
                ids = []
                for x in dsts:
                    rid, pid, _ = topo.addr(x)
                    ids.append(DstId(rid=rid, pnc=pid))
                sem = T.sem["t%d" % j] if dsts[0] in group else T.sem[part]
                calls.append(RemoteDMATransfer(dst_ids=ids, dma_engine_mask=mask, remote_sem=sem,
                                               srcs=[ap], dsts=[ap for _ in dsts]))
                total += _count(mask)
            g.remote_dma_fused(calls, local_sem=T.sem.sent)
    if total:
        g.wait_ge(T.sem.sent, total)


def rank_program(g, core, T, topo):
    acts, arrive, eta, feed = make_plan(list(T.cores), topo)
    me = T.rank_of(core)
    if me is None:
        if core in acts:
            _send(g, T, topo, acts[core], None, feed[core])
        return
    S = T.sem
    own = slice(me * NC, (me + 1) * NC)

    g.sync.dma_start(T.xb[:], T.x[:]).then_inc(S.ldx, 16)
    g.scalar.dma_start(T.ub[:], T.u[:]).then_inc(S.ldu, 16)
    g.sync.dma_start(T.vb[:], T.v[:]).then_inc(S.ldv, 16)
    g.vector.wait_ge(S.ldx, 16)
    g.vector.quantize_mx(T.qx[:, own], T.sx[:, own], T.xb[:]).then_inc(S.qx, 1)
    g.vector.wait_ge(S.ldu, 16)
    g.vector.quantize_mx(T.qu[:], T.su[:], T.ub[:]).then_inc(S.qw, 1)
    g.vector.wait_ge(S.ldv, 16)
    g.vector.quantize_mx(T.qv[:], T.sv[:], T.vb[:]).then_inc(S.qw, 1)

    g.wait_ge(S.qx, 1)
    _send(g, T, topo, acts[core], arrive[core], None)

    order = sorted(range(N), key=lambda j: (eta[core][j], j))
    g.tensor.wait_ge(S.qw, 2)
    for p, j in enumerate(order):
        cols = slice(j * NC, (j + 1) * NC)
        pos = slice(p * NC, (p + 1) * NC)
        bu = ((2 * p) % NBANKS) * BANK
        bv = ((2 * p + 1) % NBANKS) * BANK
        if j == me:
            g.tensor.wait_ge(S.qx, 1)
        else:
            g.tensor.wait_ge(S["t%d" % j], arrive[core][j])
        if 2 * p >= NBANKS:
            g.tensor.wait_ge(S["ml%d" % (p - NBANKS // 2)], 1)
        g.tensor.matmul_mx(T.ps[:, bu:bu + NC], T.qu[:], T.su[:], T.qx[:, cols], T.sx[:, cols],
                           True, True).then_inc(S["mu%d" % p], 1)
        g.tensor.matmul_mx(T.ps[:, bv:bv + NC], T.qv[:], T.sv[:], T.qx[:, cols], T.sx[:, cols],
                           True, True).then_inc(S["mv%d" % p], 1)
        g.scalar.wait_ge(S["mu%d" % p], 1)
        g.scalar.activation(T.rl[:, pos], T.ps[:, bu:bu + NC], ActivationFunctionType.Relu).then_inc(S["rs%d" % p], 1)
        g.vector.wait_ge(S["mv%d" % p], 1)
        g.vector.wait_ge(S["rs%d" % p], 1)
        g.vector.tensor_tensor(T.yb[:, cols], T.rl[:, pos], T.ps[:, bv:bv + NC], AluOpType.mult).then_inc(S["ml%d" % p], 1)

    stores = 0
    done = 0
    for upto in FLUSH:
        for p in range(done, upto):
            g.sync.wait_ge(S["ml%d" % p], 1)
        blocks = sorted(order[done:upto])
        done = upto
        run = [blocks[0], blocks[0]]
        runs = [run]
        for j in blocks[1:]:
            if j == run[1] + 1:
                run[1] = j
            else:
                run = [j, j]
                runs.append(run)
        for lo, hi in runs:
            g.sync.dma_start(T.y[:, lo * NC:(hi + 1) * NC], T.yb[:, lo * NC:(hi + 1) * NC]).then_inc(S.st, 16)
            stores += 1
    g.sync.wait_ge(S.st, 16 * stores)
